import numpy as np
import ml_dtypes


def mxq(x, axis, fmt="e4m3"):
    dtype, down = {"e4m3": (ml_dtypes.float8_e4m3fn, 7), "e5m2": (ml_dtypes.float8_e5m2, 14)}[fmt]
    v = np.moveaxis(np.asarray(x, np.float32).astype(ml_dtypes.bfloat16).astype(np.float64), axis, -1)
    blocks = v.reshape(v.shape[:-1] + (-1, 32))
    amax = np.abs(blocks).max(-1, keepdims=True)
    byte = np.maximum(np.where(amax > 0, np.frexp(amax)[1] - 1 + 127, 0) - down, 1)
    scale = np.exp2(byte - 127.0)
    codes = (blocks / scale).astype(np.float32).astype(dtype).astype(np.float64)
    return np.moveaxis((codes * scale).reshape(v.shape), -1, axis)


WIDE = False


def mx_kscale(k):
    if not WIDE:
        return np.ones(k)
    levels = np.array([10, -10, 5, -5, 0])
    if k % 512:
        return np.exp2(np.random.permutation(np.resize(levels, k // 32))).repeat(32)
    a = np.empty((k // 512, 16))
    for p in range(k // 512):
        a[p, :8] = np.random.permutation(np.resize(levels, 8))
        for g in range(8):
            far = levels[np.abs(levels - a[p, g]) >= 10]
            a[p, g + 8] = far[np.random.randint(len(far))]
    return np.exp2(a.ravel()).repeat(32)


def f64(x):
    return np.asarray(x).astype(np.float64)


def striped(idx):
    return np.tile(np.asarray(idx).reshape(-1, 16).T, (8, 1)).astype(np.uint16)


def unstriped(offs):
    return offs[:16].T.reshape(-1).astype(np.int64)


E2M1 = np.array([0.0, 0.5, 1.0, 1.5, 2.0, 3.0, 4.0, 6.0, -0.0, -0.5, -1.0, -1.5, -2.0, -3.0, -4.0, -6.0])


def pack_weight(w, fmt):
    k, n = w.shape
    w = f64(np.asarray(w, np.float32).astype(ml_dtypes.bfloat16)).reshape(k // 32, 32, n)
    amax = np.abs(w).max(1)
    if fmt == "e4m3":
        byte = np.frexp(amax)[1] - 1 + 127 - 7
    else:
        mant, ex = np.frexp(amax / 6.0)
        byte = np.where(mant > 0.5, ex, ex - 1) + 127
    byte = np.clip(np.where(amax > 0, byte, 1), 1, 254)
    scaled = (w * np.exp2(127.0 - byte)[:, None, :]).reshape(k, n).astype(np.float32)
    by_word = np.ascontiguousarray(scaled.reshape(k // 512, 128, 4, n).transpose(0, 1, 3, 2))
    if fmt == "e4m3":
        words = by_word.astype(ml_dtypes.float8_e4m3fn).view(np.uint8)
    else:
        c = by_word.astype(ml_dtypes.float4_e2m1fn).view(np.uint8) & 0xF
        words = (c[..., 0::2] | (c[..., 1::2] << 4)).reshape(k // 512, 128, 2 * n)
    return np.ascontiguousarray(words), np.ascontiguousarray(byte.astype(np.uint8).reshape(k // 512, 16, n))


def unpack_weight(words, scales, fmt):
    g, _, n = scales.shape
    words = np.ascontiguousarray(words).reshape(g, 128, n, -1)
    if fmt == "e4m3":
        vals = words.view(ml_dtypes.float8_e4m3fn).astype(np.float64)
    else:
        nib = np.empty((g, 128, n, 4), np.uint8)
        nib[..., 0::2] = words & 0xF
        nib[..., 1::2] = words >> 4
        vals = E2M1[nib]
    vals = vals * np.repeat(np.exp2(scales.astype(np.float64) - 127.0), 8, axis=1)[..., None]
    return vals.transpose(0, 1, 3, 2).reshape(g * 512, n)


def sigmoid(v):
    return 1.0 / (1.0 + np.exp(-v))


D, T, I, Q, E, U, M = 512, 2048, 512, 512, 512, 1024, 1024


def setup_inputs():
    n = np.random.standard_normal
    idx = np.random.permutation(T)[:I]
    idx2 = np.random.permutation(U)[:Q]
    idx3 = np.random.permutation(M)[:I]
    fd = mx_kscale(D)
    fq = mx_kscale(Q)
    keysp = pack_weight(n((D, T)) / fd[:, None], "e4m3")
    return {
        "users": (n((D, U)) * 1.0 / np.sqrt(D) * fd[:, None]).astype(np.float32),
        "keys_words": keysp[0],
        "keys_scales": keysp[1],
        "qs": (np.random.uniform(0.5, 2.0, (Q, 1)) * fq[:, None]).astype(np.float32),
        "msgs": (n((Q, E)) * 1 / np.sqrt(Q) / fq[:, None]).astype(np.float32),
        "old": (n((E, M)) * 1.0).astype(np.float32),
        "fade": (np.random.uniform(0.3, 0.9, (1, M))).astype(np.float32),
        "offs": striped(idx),
        "offs2": striped(idx2),
        "offs3": striped(idx3),
    }


def reference(users, keys_words, keys_scales, qs, msgs, old, fade, offs, offs2, offs3):
    idx = unstriped(offs)
    idx2 = unstriped(offs2)
    idx3 = unstriped(offs3)
    keysu = unpack_weight(keys_words, keys_scales, "e4m3")
    usersidx2q = mxq(f64(users)[:, idx2], 0, "e4m3")
    keysidxg = keysu[:, idx]
    s = usersidx2q.T @ keysidxg
    w = sigmoid(s)
    wq = w * f64(qs)
    msgsq = mxq(f64(msgs), 0, "e4m3")
    wqq = mxq(wq, 0, "e4m3")
    dl = msgsq.T @ wqq
    df = np.zeros((E, M))
    df[:, idx3] = dl
    y = f64(old) * f64(fade) + df
    return y

@@ -1,0 +1,234 @@
+from contextlib import ExitStack
+
+import concourse.mybir as mybir
+from concourse.masks import make_identity
+
+D, T, I, Q, E, U, M = 512, 2048, 512, 512, 512, 1024, 1024
+FLOPS = 2 * D * Q * I + 2 * Q * E * I
+
+F32 = mybir.dt.float32
+BF16 = mybir.dt.bfloat16
+I32 = mybir.dt.int32
+U32 = mybir.dt.uint32
+U16 = mybir.dt.uint16
+U8 = mybir.dt.uint8
+FP8X4 = mybir.dt.float8_e4m3fn_x4
+MULT = mybir.AluOpType.mult
+ADD = mybir.AluOpType.add
+COPY = mybir.ActivationFunctionType.Copy
+SIGMOID = mybir.ActivationFunctionType.Sigmoid
+
+P = 128
+PACK = 4
+CH = 128
+NCH = I // CH
+LIST = 16
+EA = 128
+
+
+def tile_attend_listedqueries_delivered_lean_kernel(
+    tc, users, keys_words, keys_scales, qs, msgs, old, fade, offs, offs2, offs3, out
+):
+    nc = tc.nc
+    with ExitStack() as ctx:
+        sb = ctx.enter_context(tc.tile_pool(name="sb", bufs=1))
+        ps_fade = ctx.enter_context(tc.psum_pool(name="ps_fade", bufs=1))
+        ps_s = ctx.enter_context(tc.psum_pool(name="ps_s", bufs=4))
+        ps_d = ctx.enter_context(tc.psum_pool(name="ps_d", bufs=2))
+
+        key_list = sb.tile([P, I // LIST], U16, name="key_list")
+        user_list = sb.tile([P, Q // LIST], U16, name="user_list")
+        place_list = sb.tile([P, I // LIST], U16, name="place_list")
+        user_pool = [sb.tile([P, U], F32, name=f"user_pool{t}") for t in range(PACK)]
+        key_words = sb.tile([P, T], U32, name="key_words")
+        key_bytes = sb.tile([P, T], U8, name="key_bytes")
+        qs_sb = sb.tile([P, PACK], F32, name="qs_sb")
+        fade_cols = sb.tile([P, 2, PACK], F32, name="fade_cols")
+        msgs_a = sb.tile([P, PACK, EA], F32, name="msgs_a")
+        msgs_b = sb.tile([P, PACK, E - EA], F32, name="msgs_b")
+        old_sb = [sb.tile([P, M], F32, name=f"old_sb{j}") for j in range(4)]
+        placed = [sb.tile([P, M], F32, name=f"placed{j}") for j in range(4)]
+        ident = sb.tile([P, P], F32, name="ident")
+
+        nc.vector.memset(key_bytes[:].bitcast(I32), 0)
+        users_by_plane = users.rearrange("(p t) u -> t p u", t=PACK)
+        scale_rows = keys_scales[0].rearrange("(g r) n -> r g n", r=4)
+        msgs_rows = msgs.rearrange("(p r) e -> p r e", r=PACK)
+        nc.sync.dma_start(user_pool[0][:], users_by_plane[0])
+        nc.sync.dma_start(user_list[:], offs2)
+        nc.sync.dma_start(user_pool[1][:], users_by_plane[1])
+        nc.sync.dma_start(key_list[:], offs)
+        for r in range(4):
+            nc.scalar.dma_start(key_bytes[r:P:32, :].bitcast(I32), scale_rows[r].bitcast(I32))
+        nc.sync.dma_start(user_pool[2][:], users_by_plane[2])
+        nc.sync.dma_start(user_pool[3][:], users_by_plane[3])
+        nc.sync.dma_start(
+            key_words[:].bitcast(I32), keys_words[0].rearrange("p n t -> p (n t)").bitcast(I32)
+        )
+        nc.sync.dma_start(msgs_a[:], msgs_rows[:, :, 0:EA])
+        nc.sync.dma_start(qs_sb[:], qs.rearrange("(p r) o -> p (r o)", r=PACK))
+        nc.sync.dma_start(msgs_b[:], msgs_rows[:, :, EA:E])
+        nc.sync.dma_start(fade_cols[:], fade.rearrange("o (h p c) -> p (o h) c", h=2, c=PACK))
+        nc.sync.dma_start(place_list[:], offs3)
+        for j in (0, 1, 3, 2):
+            nc.sync.dma_start(old_sb[j][:], old[j * P : (j + 1) * P, :])
+
+        make_identity(nc, ident[:])
+        for j in range(4):
+            nc.gpsimd.memset(placed[j][:], 0.0)
+
+        planes = sb.tile([P, PACK, Q], BF16, name="planes")
+        half = Q // 2
+        got_bytes = sb.tile([P, I], U8, name="got_bytes", align_bytes=64)
+        for t in range(PACK):
+            nc.vector.tensor_copy(
+                planes[:, t, 0:half], user_pool[t][:].indirect(user_list[:, 0 : half // LIST])
+            )
+            nc.scalar.activation(
+                planes[:, t, half:Q], user_pool[t][:].indirect(user_list[:, half // LIST : Q // LIST]), COPY
+            )
+            if t == 1:
+                nc.vector.tensor_copy(got_bytes[:], key_bytes[:].indirect(key_list[:]))
+        u_woven = sb.tile([P, Q * PACK], BF16, name="u_woven", align_bytes=64)
+        woven_view = u_woven[:].rearrange("p (r a b t) -> p a r b t", r=PACK, b=2, t=PACK)
+        planes_view = planes[:].rearrange("p t (a b r) -> p a r b t", b=2, r=PACK)
+        nc.vector.tensor_copy(woven_view[:, 0:44], planes_view[:, 0:44])
+        nc.scalar.copy(woven_view[:, 44:64], planes_view[:, 44:64])
+        got_words = [sb.tile([P, CH], U32, name=f"got_words{c}", align_bytes=64) for c in range(NCH)]
+
+        def gather_words(c):
+            nc.vector.tensor_copy(
+                got_words[c][:], key_words[:].indirect(key_list[:, c * CH // LIST : (c + 1) * CH // LIST])
+            )
+
+        gather_words(0)
+        u_codes = sb.tile([P, Q], U32, name="u_codes", align_bytes=64)
+        u_scales = sb.tile([P, Q], U8, name="u_scales", align_bytes=64)
+        nc.vector.quantize_mx(out=u_codes[:].bitcast(FP8X4), scales=u_scales[:], in_=u_woven[:])
+
+        ma_woven = sb.tile([P, EA * PACK], BF16, name="ma_woven", align_bytes=64)
+        mb_woven = sb.tile([P, (E - EA) * PACK], BF16, name="mb_woven", align_bytes=64)
+        ma_codes = sb.tile([P, EA], U32, name="ma_codes", align_bytes=64)
+        ma_scales = sb.tile([P, EA], U8, name="ma_scales", align_bytes=64)
+        mb_codes = sb.tile([P, E - EA], U32, name="mb_codes", align_bytes=64)
+        mb_scales = sb.tile([P, E - EA], U8, name="mb_scales", align_bytes=64)
+        nc.scalar.copy(ma_woven[:].rearrange("p (e r) -> p e r", r=PACK), msgs_a[:].rearrange("p r e -> p e r"))
+
+        for c in range(1, NCH):
+            gather_words(c)
+        nc.vector.quantize_mx(out=ma_codes[:].bitcast(FP8X4), scales=ma_scales[:], in_=ma_woven[:])
+
+        def m_operand(j):
+            if j * P < EA:
+                return ma_codes[:, j * P : (j + 1) * P], ma_scales[:, j * P : (j + 1) * P]
+            return mb_codes[:, j * P - EA : (j + 1) * P - EA], mb_scales[:, j * P - EA : (j + 1) * P - EA]
+
+        dl = [sb.tile([P, I], F32, name=f"dl{j}") for j in range(4)]
+
+        def scatter(engine, j, a, b):
+            window = placed[j][:].indirect(place_list[:, a // LIST : b // LIST])
+            if engine == "s":
+                nc.scalar.activation(window, dl[j][:, a:b], COPY)
+            else:
+                nc.vector.tensor_copy(window, dl[j][:, a:b])
+
+        w = sb.tile([P, NCH * CH * PACK], F32, name="w", tag="w_then_faded")
+        w_codes = sb.tile([P, I], U32, name="w_codes", align_bytes=64)
+        w_scales = sb.tile([P, I], U8, name="w_scales", align_bytes=64)
+        for c in range(NCH):
+            cols = slice(c * CH, (c + 1) * CH)
+            s_bank = ps_s.tile([P, PACK, CH], F32, name="s_bank", tag="bank")
+            for r in range(PACK):
+                nc.tensor.matmul_mx(
+                    out=s_bank[:, r, :],
+                    lhsT=u_codes[:, r * P : (r + 1) * P].bitcast(FP8X4),
+                    lhsT_scale=u_scales[:, r * P : (r + 1) * P],
+                    rhs=got_words[c][:].bitcast(FP8X4),
+                    rhs_scale=got_bytes[:, cols],
+                    start=True,
+                    stop=True,
+                )
+            w_c = w[:, c * CH * PACK : (c + 1) * CH * PACK].rearrange("p (i r) -> p i r", r=PACK)
+            nc.scalar.activation(w_c, s_bank[:].rearrange("p r i -> p i r"), SIGMOID)
+            wq = sb.tile([P, CH * PACK], BF16, name=f"wq{c}", align_bytes=64)
+            nc.vector.tensor_tensor(
+                wq[:].rearrange("p (i r) -> p i r", r=PACK),
+                w_c,
+                qs_sb[:].unsqueeze(1).to_broadcast([P, CH, PACK]),
+                MULT,
+            )
+            nc.vector.quantize_mx(out=w_codes[:, cols].bitcast(FP8X4), scales=w_scales[:, cols], in_=wq[:])
+            d_bank = ps_d.tile([P, CH], F32, name="d_bank")
+            codes, scales = m_operand(0)
+            nc.tensor.matmul_mx(
+                out=d_bank[:],
+                lhsT=codes.bitcast(FP8X4),
+                lhsT_scale=scales,
+                rhs=w_codes[:, cols].bitcast(FP8X4),
+                rhs_scale=w_scales[:, cols],
+                start=True,
+                stop=True,
+            )
+            nc.scalar.copy(dl[0][:, cols], d_bank[:])
+            scatter("s", 0, c * CH, (c + 1) * CH)
+            if c == 0:
+                nc.vector.tensor_copy(
+                    mb_woven[:].rearrange("p (e r) -> p e r", r=PACK), msgs_b[:].rearrange("p r e -> p e r")
+                )
+            if c == 0 + 1:
+                nc.vector.quantize_mx(out=mb_codes[:].bitcast(FP8X4), scales=mb_scales[:], in_=mb_woven[:])
+
+        fade_bank = [ps_fade.tile([P, PACK, P], F32, name=f"fade_bank{h}") for h in range(2)]
+        for h in range(2):
+            for c in range(PACK):
+                nc.tensor.transpose(
+                    fade_bank[h][:, c, :], fade_cols[:, h, c : c + 1].to_broadcast([P, P]), ident[:]
+                )
+
+        banks = {}
+        for j in (3, 1, 2):
+            banks[j] = ps_s.tile([P, I], F32, name=f"d_whole{j}", tag="bank")
+            codes, scales = m_operand(j)
+            nc.tensor.matmul_mx(
+                out=banks[j][:],
+                lhsT=codes.bitcast(FP8X4),
+                lhsT_scale=scales,
+                rhs=w_codes[:].bitcast(FP8X4),
+                rhs_scale=w_scales[:],
+                start=True,
+                stop=True,
+            )
+
+        faded = sb.tile([P, 4 * M], F32, name="faded", tag="w_then_faded")
+
+        def fade_tile(j):
+            for h in range(2):
+                src = old_sb[j][:, h * 512 : (h + 1) * 512].rearrange("p (n c) -> p n c", c=PACK)
+                dst = faded[:, j * M + h * 512 : j * M + (h + 1) * 512].rearrange("p (n c) -> p n c", c=PACK)
+                nc.vector.tensor_tensor(dst, src, fade_bank[h][:].rearrange("p c n -> p n c"), MULT)
+
+        def finish(engine, j, a, b, onto=None):
+            eng = nc.gpsimd if engine == "g" else nc.vector
+            result = old_sb[j][:, a:b] if onto is None else faded[:, onto * M + a : onto * M + b]
+            eng.tensor_tensor(result, faded[:, j * M + a : j * M + b], placed[j][:, a:b], ADD)
+            nc.sync.dma_start(out[j * P : (j + 1) * P, a:b], result)
+
+        for step in [
+            ("fade", 0), ("finish", "g", 0, 0, 1024), ("fade", 1),
+            ("copy", "s", 3), ("copy", "s", 1), ("scatter", "s", 1, 0, 256), ("scatter", "s", 1, 256, 512),
+            ("copy", "s", 2), ("scatter", "s", 2, 0, 256), ("scatter", "s", 2, 256, 512),
+            ("scatter", "v", 3, 0, 512), ("finish", "g", 1, 0, 1024), ("fade", 3), ("fade", 2),
+            ("finish", "v", 3, 0, 1024, 1),
+            ("finish", "v", 2, 0, 512), ("finish", "v", 2, 512, 768), ("finish", "v", 2, 768, 1024),
+        ]:
+            if step[0] == "fade":
+                fade_tile(step[1])
+            elif step[0] == "copy":
+                if step[1] == "s":
+                    nc.scalar.copy(dl[step[2]][:], banks[step[2]][:])
+                else:
+                    nc.vector.tensor_copy(dl[step[2]][:], banks[step[2]][:])
+            elif step[0] == "scatter":
+                scatter(*step[1:])
+            else:
+                finish(*step[1:])

@@ -23,7 +23,7 @@ PACK = 4
 CH = 128
 NCH = I // CH
 LIST = 16
-EA = 128
+EA = 256
 
 
 def tile_attend_listedqueries_delivered_lean_kernel(
@@ -50,16 +50,17 @@ def tile_attend_listedqueries_delivered_lean_kernel(
         placed = [sb.tile([P, M], F32, name=f"placed{j}") for j in range(4)]
         ident = sb.tile([P, P], F32, name="ident")
 
-        nc.vector.memset(key_bytes[:].bitcast(I32), 0)
+        nc.gpsimd.memset(key_bytes[:].bitcast(I32), 0)
         users_by_plane = users.rearrange("(p t) u -> t p u", t=PACK)
         scale_rows = keys_scales[0].rearrange("(g r) n -> r g n", r=4)
         msgs_rows = msgs.rearrange("(p r) e -> p r e", r=PACK)
-        nc.sync.dma_start(user_pool[0][:], users_by_plane[0])
+        nc.sync.dma_start(fade_cols[:], fade.rearrange("o (h p c) -> p (o h) c", h=2, c=PACK))
         nc.sync.dma_start(user_list[:], offs2)
+        nc.sync.dma_start(user_pool[0][:], users_by_plane[0])
         nc.sync.dma_start(user_pool[1][:], users_by_plane[1])
         nc.sync.dma_start(key_list[:], offs)
         for r in range(4):
-            nc.scalar.dma_start(key_bytes[r:P:32, :].bitcast(I32), scale_rows[r].bitcast(I32))
+            nc.sync.dma_start(key_bytes[r:P:32, :].bitcast(I32), scale_rows[r].bitcast(I32))
         nc.sync.dma_start(user_pool[2][:], users_by_plane[2])
         nc.sync.dma_start(user_pool[3][:], users_by_plane[3])
         nc.sync.dma_start(
@@ -68,14 +69,30 @@ def tile_attend_listedqueries_delivered_lean_kernel(
         nc.sync.dma_start(msgs_a[:], msgs_rows[:, :, 0:EA])
         nc.sync.dma_start(qs_sb[:], qs.rearrange("(p r) o -> p (r o)", r=PACK))
         nc.sync.dma_start(msgs_b[:], msgs_rows[:, :, EA:E])
-        nc.sync.dma_start(fade_cols[:], fade.rearrange("o (h p c) -> p (o h) c", h=2, c=PACK))
         nc.sync.dma_start(place_list[:], offs3)
-        for j in (0, 1, 3, 2):
+        for j in (3, 0, 1, 2):
             nc.sync.dma_start(old_sb[j][:], old[j * P : (j + 1) * P, :])
 
+        warm = sb.tile([P, 16], F32, name="warm")
+        nc.vector.memset(warm[:, 0:8], 0.0)
+        nc.scalar.activation(warm[:, 8:16], warm[:, 0:8], SIGMOID)
         make_identity(nc, ident[:])
         for j in range(4):
-            nc.gpsimd.memset(placed[j][:], 0.0)
+            (nc.vector if j < 2 else nc.gpsimd).memset(placed[j][:], 0.0)
+
+        fade_bank = [ps_fade.tile([P, PACK, P], F32, name=f"fade_bank{h}") for h in range(2)]
+        for h in range(2):
+            for c in range(PACK):
+                nc.tensor.transpose(
+                    fade_bank[h][:, c, :], fade_cols[:, h, c : c + 1].to_broadcast([P, P]), ident[:]
+                )
+
+        fade_row = sb.tile([P, M], F32, name="fade_row")
+        for h in range(2):
+            nc.scalar.copy(
+                fade_row[:, h * 512 : (h + 1) * 512].rearrange("p (n c) -> p n c", c=PACK),
+                fade_bank[h][:].rearrange("p c n -> p n c"),
+            )
 
         planes = sb.tile([P, PACK, Q], BF16, name="planes")
         half = Q // 2
@@ -87,13 +104,14 @@ def tile_attend_listedqueries_delivered_lean_kernel(
             nc.scalar.activation(
                 planes[:, t, half:Q], user_pool[t][:].indirect(user_list[:, half // LIST : Q // LIST]), COPY
             )
-            if t == 1:
-                nc.vector.tensor_copy(got_bytes[:], key_bytes[:].indirect(key_list[:]))
+            if t in (1, 2):
+                a, b = (t - 1) * half, t * half
+                nc.vector.tensor_copy(got_bytes[:, a:b], key_bytes[:].indirect(key_list[:, a // LIST : b // LIST]))
         u_woven = sb.tile([P, Q * PACK], BF16, name="u_woven", align_bytes=64)
         woven_view = u_woven[:].rearrange("p (r a b t) -> p a r b t", r=PACK, b=2, t=PACK)
         planes_view = planes[:].rearrange("p t (a b r) -> p a r b t", b=2, r=PACK)
-        nc.vector.tensor_copy(woven_view[:, 0:44], planes_view[:, 0:44])
-        nc.scalar.copy(woven_view[:, 44:64], planes_view[:, 44:64])
+        nc.vector.tensor_copy(woven_view[:, 0:46], planes_view[:, 0:46])
+        nc.scalar.copy(woven_view[:, 46:64], planes_view[:, 46:64])
         got_words = [sb.tile([P, CH], U32, name=f"got_words{c}", align_bytes=64) for c in range(NCH)]
 
         def gather_words(c):
@@ -101,21 +119,30 @@ def tile_attend_listedqueries_delivered_lean_kernel(
                 got_words[c][:], key_words[:].indirect(key_list[:, c * CH // LIST : (c + 1) * CH // LIST])
             )
 
-        gather_words(0)
         u_codes = sb.tile([P, Q], U32, name="u_codes", align_bytes=64)
         u_scales = sb.tile([P, Q], U8, name="u_scales", align_bytes=64)
-        nc.vector.quantize_mx(out=u_codes[:].bitcast(FP8X4), scales=u_scales[:], in_=u_woven[:])
+        for a in (0, half):
+            nc.vector.quantize_mx(
+                out=u_codes[:, a : a + half].bitcast(FP8X4),
+                scales=u_scales[:, a : a + half],
+                in_=u_woven[:, a * PACK : (a + half) * PACK],
+            )
+            if a == 0:
+                gather_words(0)
 
         ma_woven = sb.tile([P, EA * PACK], BF16, name="ma_woven", align_bytes=64)
-        mb_woven = sb.tile([P, (E - EA) * PACK], BF16, name="mb_woven", align_bytes=64)
+        late_in = sb.tile([P, (I + E - EA) * PACK], BF16, name="late_in", tag="late_in_then_faded", align_bytes=64)
+        mb_woven = late_in[:, I * PACK : (I + E - EA) * PACK]
         ma_codes = sb.tile([P, EA], U32, name="ma_codes", align_bytes=64)
         ma_scales = sb.tile([P, EA], U8, name="ma_scales", align_bytes=64)
         mb_codes = sb.tile([P, E - EA], U32, name="mb_codes", align_bytes=64)
         mb_scales = sb.tile([P, E - EA], U8, name="mb_scales", align_bytes=64)
-        nc.scalar.copy(ma_woven[:].rearrange("p (e r) -> p e r", r=PACK), msgs_a[:].rearrange("p r e -> p e r"))
 
         for c in range(1, NCH):
             gather_words(c)
+        nc.vector.tensor_copy(
+            ma_woven[:].rearrange("p (e r) -> p e r", r=PACK), msgs_a[:].rearrange("p r e -> p e r")
+        )
         nc.vector.quantize_mx(out=ma_codes[:].bitcast(FP8X4), scales=ma_scales[:], in_=ma_woven[:])
 
         def m_operand(j):
@@ -123,7 +150,10 @@ def tile_attend_listedqueries_delivered_lean_kernel(
                 return ma_codes[:, j * P : (j + 1) * P], ma_scales[:, j * P : (j + 1) * P]
             return mb_codes[:, j * P - EA : (j + 1) * P - EA], mb_scales[:, j * P - EA : (j + 1) * P - EA]
 
-        dl = [sb.tile([P, I], F32, name=f"dl{j}") for j in range(4)]
+        dl_all = sb.tile([P, 3, I], F32, name="dl_all")
+        dl_last = sb.tile([P, M], F32, name="dl_last")
+        dl = [dl_all[:, 0, :], dl_all[:, 1, :], dl_all[:, 2, :], dl_last[:, 0:I]]
+        stretch = {0: (0, 128), 1: (128, 256), 3: (256, 512)}
 
         def scatter(engine, j, a, b):
             window = placed[j][:].indirect(place_list[:, a // LIST : b // LIST])
@@ -150,27 +180,33 @@ def tile_attend_listedqueries_delivered_lean_kernel(
                 )
             w_c = w[:, c * CH * PACK : (c + 1) * CH * PACK].rearrange("p (i r) -> p i r", r=PACK)
             nc.scalar.activation(w_c, s_bank[:].rearrange("p r i -> p i r"), SIGMOID)
-            wq = sb.tile([P, CH * PACK], BF16, name=f"wq{c}", align_bytes=64)
+            wq = late_in[:, c * CH * PACK : (c + 1) * CH * PACK]
             nc.vector.tensor_tensor(
                 wq[:].rearrange("p (i r) -> p i r", r=PACK),
                 w_c,
                 qs_sb[:].unsqueeze(1).to_broadcast([P, CH, PACK]),
                 MULT,
             )
-            nc.vector.quantize_mx(out=w_codes[:, cols].bitcast(FP8X4), scales=w_scales[:, cols], in_=wq[:])
-            d_bank = ps_d.tile([P, CH], F32, name="d_bank")
-            codes, scales = m_operand(0)
-            nc.tensor.matmul_mx(
-                out=d_bank[:],
-                lhsT=codes.bitcast(FP8X4),
-                lhsT_scale=scales,
-                rhs=w_codes[:, cols].bitcast(FP8X4),
-                rhs_scale=w_scales[:, cols],
-                start=True,
-                stop=True,
-            )
-            nc.scalar.copy(dl[0][:, cols], d_bank[:])
-            scatter("s", 0, c * CH, (c + 1) * CH)
+            if c in stretch:
+                a, b = stretch[c]
+                nc.vector.quantize_mx(
+                    out=w_codes[:, a:b].bitcast(FP8X4), scales=w_scales[:, a:b], in_=late_in[:, a * PACK : b * PACK]
+                )
+                d_bank = ps_d.tile([P, 2, b - a], F32, name="d_bank")
+                for j in range(2):
+                    codes, scales = m_operand(j)
+                    nc.tensor.matmul_mx(
+                        out=d_bank[:, j, :],
+                        lhsT=codes.bitcast(FP8X4),
+                        lhsT_scale=scales,
+                        rhs=w_codes[:, a:b].bitcast(FP8X4),
+                        rhs_scale=w_scales[:, a:b],
+                        start=True,
+                        stop=True,
+                    )
+                nc.scalar.copy(dl_all[:, 0:2, a:b], d_bank[:])
+                for j in range(2):
+                    scatter("s", j, a, b)
             if c == 0:
                 nc.vector.tensor_copy(
                     mb_woven[:].rearrange("p (e r) -> p e r", r=PACK), msgs_b[:].rearrange("p r e -> p e r")
@@ -178,15 +214,8 @@ def tile_attend_listedqueries_delivered_lean_kernel(
             if c == 0 + 1:
                 nc.vector.quantize_mx(out=mb_codes[:].bitcast(FP8X4), scales=mb_scales[:], in_=mb_woven[:])
 
-        fade_bank = [ps_fade.tile([P, PACK, P], F32, name=f"fade_bank{h}") for h in range(2)]
-        for h in range(2):
-            for c in range(PACK):
-                nc.tensor.transpose(
-                    fade_bank[h][:, c, :], fade_cols[:, h, c : c + 1].to_broadcast([P, P]), ident[:]
-                )
-
         banks = {}
-        for j in (3, 1, 2):
+        for j in (3, 2):
             banks[j] = ps_s.tile([P, I], F32, name=f"d_whole{j}", tag="bank")
             codes, scales = m_operand(j)
             nc.tensor.matmul_mx(
@@ -199,35 +228,42 @@ def tile_attend_listedqueries_delivered_lean_kernel(
                 stop=True,
             )
 
-        faded = sb.tile([P, 4 * M], F32, name="faded", tag="w_then_faded")
+        faded_v = sb.tile([P, 2 * M], F32, name="faded_v", tag="w_then_faded")
+        faded_g = sb.tile([P, 2 * M], F32, name="faded_g", tag="late_in_then_faded", align_bytes=64)
+        faded = {3: faded_v[:, 0:M], 0: faded_v[:, M : 2 * M], 1: faded_g[:, 0:M], 2: faded_g[:, M : 2 * M], 4: dl_last[:]}
 
-        def fade_tile(j):
+        def fade_tile(engine, j):
+            if engine == "g":
+                nc.gpsimd.tensor_tensor(faded[j], old_sb[j][:], fade_row[:], MULT)
+                return
             for h in range(2):
                 src = old_sb[j][:, h * 512 : (h + 1) * 512].rearrange("p (n c) -> p n c", c=PACK)
-                dst = faded[:, j * M + h * 512 : j * M + (h + 1) * 512].rearrange("p (n c) -> p n c", c=PACK)
+                dst = faded[j][:, h * 512 : (h + 1) * 512].rearrange("p (n c) -> p n c", c=PACK)
                 nc.vector.tensor_tensor(dst, src, fade_bank[h][:].rearrange("p c n -> p n c"), MULT)
 
         def finish(engine, j, a, b, onto=None):
             eng = nc.gpsimd if engine == "g" else nc.vector
-            result = old_sb[j][:, a:b] if onto is None else faded[:, onto * M + a : onto * M + b]
-            eng.tensor_tensor(result, faded[:, j * M + a : j * M + b], placed[j][:, a:b], ADD)
+            result = old_sb[j][:, a:b] if onto is None else faded[onto][:, a:b]
+            eng.tensor_tensor(result, faded[j][:, a:b], placed[j][:, a:b], ADD)
             nc.sync.dma_start(out[j * P : (j + 1) * P, a:b], result)
 
         for step in [
-            ("fade", 0), ("finish", "g", 0, 0, 1024), ("fade", 1),
-            ("copy", "s", 3), ("copy", "s", 1), ("scatter", "s", 1, 0, 256), ("scatter", "s", 1, 256, 512),
-            ("copy", "s", 2), ("scatter", "s", 2, 0, 256), ("scatter", "s", 2, 256, 512),
-            ("scatter", "v", 3, 0, 512), ("finish", "g", 1, 0, 1024), ("fade", 3), ("fade", 2),
-            ("finish", "v", 3, 0, 1024, 1),
-            ("finish", "v", 2, 0, 512), ("finish", "v", 2, 512, 768), ("finish", "v", 2, 768, 1024),
+            ("fade", "g", 1), ("fade", "g", 2),
+            ("fade", "v", 3), ("copy", "v", 3, 0, 512), ("copy", "v", 2, 0, 128), ("fade", "v", 0),
+            ("scatter", "v", 2, 0, 128), ("scatter", "v", 3, 0, 512),
+            ("copy", "s", 2, 128, 512), ("scatter", "s", 2, 128, 512),
+            ("finish", "g", 0, 0, 1024), ("finish", "g", 1, 0, 512, 0),
+            ("finish", "v", 1, 512, 1024, 0), ("finish", "v", 3, 0, 512, 1), ("finish", "v", 3, 512, 1024, 1),
+            ("finish", "v", 2, 0, 512, 3), ("finish", "v", 2, 512, 768, 3), ("finish", "v", 2, 768, 1024, 3),
         ]:
             if step[0] == "fade":
-                fade_tile(step[1])
+                fade_tile(*step[1:])
             elif step[0] == "copy":
+                j, a, b = step[2:]
                 if step[1] == "s":
-                    nc.scalar.copy(dl[step[2]][:], banks[step[2]][:])
+                    nc.scalar.copy(dl[j][:, a:b], banks[j][:, a:b])
                 else:
-                    nc.vector.tensor_copy(dl[step[2]][:], banks[step[2]][:])
+                    nc.vector.tensor_copy(dl[j][:, a:b], banks[j][:, a:b])
             elif step[0] == "scatter":
                 scatter(*step[1:])
             else:

@@ -33,7 +33,7 @@ def tile_attend_listedqueries_delivered_lean_kernel(
     with ExitStack() as ctx:
         sb = ctx.enter_context(tc.tile_pool(name="sb", bufs=1))
         ps_fade = ctx.enter_context(tc.psum_pool(name="ps_fade", bufs=1))
-        ps_s = ctx.enter_context(tc.psum_pool(name="ps_s", bufs=4))
+        ps_s = ctx.enter_context(tc.psum_pool(name="ps_s", bufs=3))
         ps_d = ctx.enter_context(tc.psum_pool(name="ps_d", bufs=2))
 
         key_list = sb.tile([P, I // LIST], U16, name="key_list")
@@ -42,7 +42,7 @@ def tile_attend_listedqueries_delivered_lean_kernel(
         user_pool = [sb.tile([P, U], F32, name=f"user_pool{t}") for t in range(PACK)]
         key_words = sb.tile([P, T], U32, name="key_words")
         key_bytes = sb.tile([P, T], U8, name="key_bytes")
-        qs_sb = sb.tile([P, PACK], F32, name="qs_sb")
+        qs_pad = sb.tile([P, P], F32, name="qs_pad")
         fade_cols = sb.tile([P, 2, PACK], F32, name="fade_cols")
         msgs_a = sb.tile([P, PACK, EA], F32, name="msgs_a")
         msgs_b = sb.tile([P, PACK, E - EA], F32, name="msgs_b")
@@ -51,6 +51,7 @@ def tile_attend_listedqueries_delivered_lean_kernel(
         ident = sb.tile([P, P], F32, name="ident")
 
         nc.gpsimd.memset(key_bytes[:].bitcast(I32), 0)
+        nc.vector.memset(qs_pad[:], 0.0)
         users_by_plane = users.rearrange("(p t) u -> t p u", t=PACK)
         scale_rows = keys_scales[0].rearrange("(g r) n -> r g n", r=4)
         msgs_rows = msgs.rearrange("(p r) e -> p r e", r=PACK)
@@ -63,14 +64,14 @@ def tile_attend_listedqueries_delivered_lean_kernel(
             nc.sync.dma_start(key_bytes[r:P:32, :].bitcast(I32), scale_rows[r].bitcast(I32))
         nc.sync.dma_start(user_pool[2][:], users_by_plane[2])
         nc.sync.dma_start(user_pool[3][:], users_by_plane[3])
+        nc.sync.dma_start(qs_pad[:, 0:PACK], qs.rearrange("(p r) o -> p (r o)", r=PACK))
         nc.sync.dma_start(
             key_words[:].bitcast(I32), keys_words[0].rearrange("p n t -> p (n t)").bitcast(I32)
         )
         nc.sync.dma_start(msgs_a[:], msgs_rows[:, :, 0:EA])
-        nc.sync.dma_start(qs_sb[:], qs.rearrange("(p r) o -> p (r o)", r=PACK))
         nc.sync.dma_start(msgs_b[:], msgs_rows[:, :, EA:E])
         nc.sync.dma_start(place_list[:], offs3)
-        for j in (3, 0, 1, 2):
+        for j in (0, 3, 1, 2):
             nc.sync.dma_start(old_sb[j][:], old[j * P : (j + 1) * P, :])
 
         warm = sb.tile([P, 16], F32, name="warm")
@@ -107,17 +108,23 @@ def tile_attend_listedqueries_delivered_lean_kernel(
             if t in (1, 2):
                 a, b = (t - 1) * half, t * half
                 nc.vector.tensor_copy(got_bytes[:, a:b], key_bytes[:].indirect(key_list[:, a // LIST : b // LIST]))
-        u_woven = sb.tile([P, Q * PACK], BF16, name="u_woven", align_bytes=64)
-        woven_view = u_woven[:].rearrange("p (r a b t) -> p a r b t", r=PACK, b=2, t=PACK)
+        late_in = sb.tile([P, (I + Q) * PACK], BF16, name="late_in", tag="late_in_then_faded", align_bytes=64)
+        u_woven = late_in[:, I * PACK : (I + Q) * PACK]
+        woven_view = u_woven.rearrange("p (r a b t) -> p a r b t", r=PACK, b=2, t=PACK)
         planes_view = planes[:].rearrange("p t (a b r) -> p a r b t", b=2, r=PACK)
         nc.vector.tensor_copy(woven_view[:, 0:46], planes_view[:, 0:46])
         nc.scalar.copy(woven_view[:, 46:64], planes_view[:, 46:64])
-        got_words = [sb.tile([P, CH], U32, name=f"got_words{c}", align_bytes=64) for c in range(NCH)]
+        qs_turned = ps_s.tile([P, P], F32, name="qs_turned", tag="bank")
+        nc.tensor.transpose(qs_turned[:], qs_pad[:], ident[:])
+        qs_rows = sb.tile([P, P], F32, name="qs_rows")
+        nc.scalar.copy(qs_rows[:], qs_turned[:])
+        qs_bank = ps_fade.tile([P, P], F32, name="qs_bank")
+        nc.tensor.transpose(qs_bank[:], qs_rows[:], ident[:])
 
-        def gather_words(c):
-            nc.vector.tensor_copy(
-                got_words[c][:], key_words[:].indirect(key_list[:, c * CH // LIST : (c + 1) * CH // LIST])
-            )
+        got_words = sb.tile([P, I], U32, name="got_words", align_bytes=64)
+
+        def gather_words(a, b):
+            nc.vector.tensor_copy(got_words[:, a:b], key_words[:].indirect(key_list[:, a // LIST : b // LIST]))
 
         u_codes = sb.tile([P, Q], U32, name="u_codes", align_bytes=64)
         u_scales = sb.tile([P, Q], U8, name="u_scales", align_bytes=64)
@@ -128,22 +135,23 @@ def tile_attend_listedqueries_delivered_lean_kernel(
                 in_=u_woven[:, a * PACK : (a + half) * PACK],
             )
             if a == 0:
-                gather_words(0)
+                gather_words(0, CH)
 
-        ma_woven = sb.tile([P, EA * PACK], BF16, name="ma_woven", align_bytes=64)
-        late_in = sb.tile([P, (I + E - EA) * PACK], BF16, name="late_in", tag="late_in_then_faded", align_bytes=64)
-        mb_woven = late_in[:, I * PACK : (I + E - EA) * PACK]
+        mb_woven = late_in[:, (I + half) * PACK : (I + Q) * PACK]
+        ma_woven = mb_woven
         ma_codes = sb.tile([P, EA], U32, name="ma_codes", align_bytes=64)
         ma_scales = sb.tile([P, EA], U8, name="ma_scales", align_bytes=64)
         mb_codes = sb.tile([P, E - EA], U32, name="mb_codes", align_bytes=64)
         mb_scales = sb.tile([P, E - EA], U8, name="mb_scales", align_bytes=64)
 
-        for c in range(1, NCH):
-            gather_words(c)
-        nc.vector.tensor_copy(
-            ma_woven[:].rearrange("p (e r) -> p e r", r=PACK), msgs_a[:].rearrange("p r e -> p e r")
+        gather_words(CH, I)
+        nc.gpsimd.tensor_scalar(
+            ma_woven.rearrange("p (e r) -> p e r", r=PACK), msgs_a[:].rearrange("p r e -> p e r"), 1.0, 0.0, MULT, ADD
         )
-        nc.vector.quantize_mx(out=ma_codes[:].bitcast(FP8X4), scales=ma_scales[:], in_=ma_woven[:])
+        nc.vector.quantize_mx(out=ma_codes[:].bitcast(FP8X4), scales=ma_scales[:], in_=ma_woven)
+        nc.gpsimd.tensor_scalar(
+            mb_woven.rearrange("p (e r) -> p e r", r=PACK), msgs_b[:].rearrange("p r e -> p e r"), 1.0, 0.0, MULT, ADD
+        )
 
         def m_operand(j):
             if j * P < EA:
@@ -158,7 +166,7 @@ def tile_attend_listedqueries_delivered_lean_kernel(
         def scatter(engine, j, a, b):
             window = placed[j][:].indirect(place_list[:, a // LIST : b // LIST])
             if engine == "s":
-                nc.scalar.activation(window, dl[j][:, a:b], COPY)
+                nc.scalar.activation(window, dl[j % 2][:, a:b], COPY)
             else:
                 nc.vector.tensor_copy(window, dl[j][:, a:b])
 
@@ -173,7 +181,7 @@ def tile_attend_listedqueries_delivered_lean_kernel(
                     out=s_bank[:, r, :],
                     lhsT=u_codes[:, r * P : (r + 1) * P].bitcast(FP8X4),
                     lhsT_scale=u_scales[:, r * P : (r + 1) * P],
-                    rhs=got_words[c][:].bitcast(FP8X4),
+                    rhs=got_words[:, cols].bitcast(FP8X4),
                     rhs_scale=got_bytes[:, cols],
                     start=True,
                     stop=True,
@@ -184,7 +192,7 @@ def tile_attend_listedqueries_delivered_lean_kernel(
             nc.vector.tensor_tensor(
                 wq[:].rearrange("p (i r) -> p i r", r=PACK),
                 w_c,
-                qs_sb[:].unsqueeze(1).to_broadcast([P, CH, PACK]),
+                qs_bank[:, 0:PACK].unsqueeze(1).to_broadcast([P, CH, PACK]),
                 MULT,
             )
             if c in stretch:
@@ -207,10 +215,6 @@ def tile_attend_listedqueries_delivered_lean_kernel(
                 nc.scalar.copy(dl_all[:, 0:2, a:b], d_bank[:])
                 for j in range(2):
                     scatter("s", j, a, b)
-            if c == 0:
-                nc.vector.tensor_copy(
-                    mb_woven[:].rearrange("p (e r) -> p e r", r=PACK), msgs_b[:].rearrange("p r e -> p e r")
-                )
             if c == 0 + 1:
                 nc.vector.quantize_mx(out=mb_codes[:].bitcast(FP8X4), scales=mb_scales[:], in_=mb_woven[:])
 
@@ -230,7 +234,7 @@ def tile_attend_listedqueries_delivered_lean_kernel(
 
         faded_v = sb.tile([P, 2 * M], F32, name="faded_v", tag="w_then_faded")
         faded_g = sb.tile([P, 2 * M], F32, name="faded_g", tag="late_in_then_faded", align_bytes=64)
-        faded = {3: faded_v[:, 0:M], 0: faded_v[:, M : 2 * M], 1: faded_g[:, 0:M], 2: faded_g[:, M : 2 * M], 4: dl_last[:]}
+        faded = {3: faded_v[:, 0:M], 0: faded_v[:, M : 2 * M], 1: faded_g[:, 0:M], 2: faded_g[:, M : 2 * M], 4: dl_last[:], 5: old_sb[2][:]}
 
         def fade_tile(engine, j):
             if engine == "g":
@@ -249,11 +253,11 @@ def tile_attend_listedqueries_delivered_lean_kernel(
 
         for step in [
             ("fade", "g", 1), ("fade", "g", 2),
-            ("fade", "v", 3), ("copy", "v", 3, 0, 512), ("copy", "v", 2, 0, 128), ("fade", "v", 0),
+            ("fade", "v", 0), ("copy", "v", 3, 0, 512), ("copy", "v", 2, 0, 128), ("fade", "v", 3),
             ("scatter", "v", 2, 0, 128), ("scatter", "v", 3, 0, 512),
             ("copy", "s", 2, 128, 512), ("scatter", "s", 2, 128, 512),
-            ("finish", "g", 0, 0, 1024), ("finish", "g", 1, 0, 512, 0),
-            ("finish", "v", 1, 512, 1024, 0), ("finish", "v", 3, 0, 512, 1), ("finish", "v", 3, 512, 1024, 1),
+            ("finish", "g", 0, 0, 1024, 5),
+            ("finish", "v", 1, 0, 1024, 0), ("finish", "v", 3, 0, 512, 1), ("finish", "v", 3, 512, 1024, 1),
             ("finish", "v", 2, 0, 512, 3), ("finish", "v", 2, 512, 768, 3), ("finish", "v", 2, 768, 1024, 3),
         ]:
             if step[0] == "fade":
@@ -261,7 +265,7 @@ def tile_attend_listedqueries_delivered_lean_kernel(
             elif step[0] == "copy":
                 j, a, b = step[2:]
                 if step[1] == "s":
-                    nc.scalar.copy(dl[j][:, a:b], banks[j][:, a:b])
+                    nc.scalar.copy(dl[j % 2][:, a:b], banks[j][:, a:b])
                 else:
                     nc.vector.tensor_copy(dl[j][:, a:b], banks[j][:, a:b])
             elif step[0] == "scatter":

from contextlib import ExitStack

import concourse.mybir as mybir
from concourse.masks import make_identity

D, T, I, Q, E, U, M = 512, 2048, 512, 512, 512, 1024, 1024
FLOPS = 2 * D * Q * I + 2 * Q * E * I

F32 = mybir.dt.float32
BF16 = mybir.dt.bfloat16
I32 = mybir.dt.int32
U32 = mybir.dt.uint32
U16 = mybir.dt.uint16
U8 = mybir.dt.uint8
FP8X4 = mybir.dt.float8_e4m3fn_x4
MULT = mybir.AluOpType.mult
ADD = mybir.AluOpType.add
COPY = mybir.ActivationFunctionType.Copy
SIGMOID = mybir.ActivationFunctionType.Sigmoid

P = 128
PACK = 4
CH = 128
NCH = I // CH
LIST = 16
EA = 256


def tile_attend_listedqueries_delivered_lean_kernel(
    tc, users, keys_words, keys_scales, qs, msgs, old, fade, offs, offs2, offs3, out
):
    nc = tc.nc
    with ExitStack() as ctx:
        sb = ctx.enter_context(tc.tile_pool(name="sb", bufs=1))
        ps_fade = ctx.enter_context(tc.psum_pool(name="ps_fade", bufs=1))
        ps_s = ctx.enter_context(tc.psum_pool(name="ps_s", bufs=3))
        ps_d = ctx.enter_context(tc.psum_pool(name="ps_d", bufs=2))

        key_list = sb.tile([P, I // LIST], U16, name="key_list")
        user_list = sb.tile([P, Q // LIST], U16, name="user_list")
        place_list = sb.tile([P, I // LIST], U16, name="place_list")
        user_pool = [sb.tile([P, U], F32, name=f"user_pool{t}") for t in range(PACK)]
        key_words = sb.tile([P, T], U32, name="key_words")
        key_bytes = sb.tile([P, T], U8, name="key_bytes")
        qs_pad = sb.tile([P, P], F32, name="qs_pad")
        fade_cols = sb.tile([P, 2, PACK], F32, name="fade_cols")
        msgs_a = sb.tile([P, PACK, EA], F32, name="msgs_a")
        msgs_b = sb.tile([P, PACK, E - EA], F32, name="msgs_b")
        old_sb = [sb.tile([P, M], F32, name=f"old_sb{j}") for j in range(4)]
        placed = [sb.tile([P, M], F32, name=f"placed{j}") for j in range(4)]
        ident = sb.tile([P, P], F32, name="ident")

        nc.gpsimd.memset(key_bytes[:].bitcast(I32), 0)
        nc.vector.memset(qs_pad[:], 0.0)
        users_by_plane = users.rearrange("(p t) u -> t p u", t=PACK)
        scale_rows = keys_scales[0].rearrange("(g r) n -> r g n", r=4)
        msgs_rows = msgs.rearrange("(p r) e -> p r e", r=PACK)
        nc.sync.dma_start(fade_cols[:], fade.rearrange("o (h p c) -> p (o h) c", h=2, c=PACK))
        nc.sync.dma_start(user_list[:], offs2)
        nc.sync.dma_start(user_pool[0][:], users_by_plane[0])
        nc.sync.dma_start(user_pool[1][:], users_by_plane[1])
        nc.sync.dma_start(key_list[:], offs)
        for r in range(4):
            nc.sync.dma_start(key_bytes[r:P:32, :].bitcast(I32), scale_rows[r].bitcast(I32))
        nc.sync.dma_start(user_pool[2][:], users_by_plane[2])
        nc.sync.dma_start(user_pool[3][:], users_by_plane[3])
        nc.sync.dma_start(qs_pad[:, 0:PACK], qs.rearrange("(p r) o -> p (r o)", r=PACK))
        nc.sync.dma_start(
            key_words[:].bitcast(I32), keys_words[0].rearrange("p n t -> p (n t)").bitcast(I32)
        )
        nc.sync.dma_start(msgs_a[:], msgs_rows[:, :, 0:EA])
        nc.sync.dma_start(msgs_b[:], msgs_rows[:, :, EA:E])
        nc.sync.dma_start(place_list[:], offs3)
        for j in (0, 3, 1, 2):
            nc.sync.dma_start(old_sb[j][:], old[j * P : (j + 1) * P, :])

        warm = sb.tile([P, 16], F32, name="warm")
        nc.vector.memset(warm[:, 0:8], 0.0)
        nc.scalar.activation(warm[:, 8:16], warm[:, 0:8], SIGMOID)
        make_identity(nc, ident[:])
        for j in range(4):
            (nc.vector if j < 2 else nc.gpsimd).memset(placed[j][:], 0.0)

        fade_bank = [ps_fade.tile([P, PACK, P], F32, name=f"fade_bank{h}") for h in range(2)]
        for h in range(2):
            for c in range(PACK):
                nc.tensor.transpose(
                    fade_bank[h][:, c, :], fade_cols[:, h, c : c + 1].to_broadcast([P, P]), ident[:]
                )

        fade_row = sb.tile([P, M], F32, name="fade_row")
        for h in range(2):
            nc.scalar.copy(
                fade_row[:, h * 512 : (h + 1) * 512].rearrange("p (n c) -> p n c", c=PACK),
                fade_bank[h][:].rearrange("p c n -> p n c"),
            )

        planes = sb.tile([P, PACK, Q], BF16, name="planes")
        half = Q // 2
        got_bytes = sb.tile([P, I], U8, name="got_bytes", align_bytes=64)
        for t in range(PACK):
            nc.vector.tensor_copy(
                planes[:, t, 0:half], user_pool[t][:].indirect(user_list[:, 0 : half // LIST])
            )
            nc.scalar.activation(
                planes[:, t, half:Q], user_pool[t][:].indirect(user_list[:, half // LIST : Q // LIST]), COPY
            )
            if t in (1, 2):
                a, b = (t - 1) * half, t * half
                nc.vector.tensor_copy(got_bytes[:, a:b], key_bytes[:].indirect(key_list[:, a // LIST : b // LIST]))
        late_in = sb.tile([P, (I + Q) * PACK], BF16, name="late_in", tag="late_in_then_faded", align_bytes=64)
        u_woven = late_in[:, I * PACK : (I + Q) * PACK]
        woven_view = u_woven.rearrange("p (r a b t) -> p a r b t", r=PACK, b=2, t=PACK)
        planes_view = planes[:].rearrange("p t (a b r) -> p a r b t", b=2, r=PACK)
        nc.vector.tensor_copy(woven_view[:, 0:46], planes_view[:, 0:46])
        nc.scalar.copy(woven_view[:, 46:64], planes_view[:, 46:64])
        qs_turned = ps_s.tile([P, P], F32, name="qs_turned", tag="bank")
        nc.tensor.transpose(qs_turned[:], qs_pad[:], ident[:])
        qs_rows = sb.tile([P, P], F32, name="qs_rows")
        nc.scalar.copy(qs_rows[:], qs_turned[:])
        qs_bank = ps_fade.tile([P, P], F32, name="qs_bank")
        nc.tensor.transpose(qs_bank[:], qs_rows[:], ident[:])

        got_words = sb.tile([P, I], U32, name="got_words", align_bytes=64)

        def gather_words(a, b):
            nc.vector.tensor_copy(got_words[:, a:b], key_words[:].indirect(key_list[:, a // LIST : b // LIST]))

        u_codes = sb.tile([P, Q], U32, name="u_codes", align_bytes=64)
        u_scales = sb.tile([P, Q], U8, name="u_scales", align_bytes=64)
        for a in (0, half):
            nc.vector.quantize_mx(
                out=u_codes[:, a : a + half].bitcast(FP8X4),
                scales=u_scales[:, a : a + half],
                in_=u_woven[:, a * PACK : (a + half) * PACK],
            )
            if a == 0:
                gather_words(0, CH)

        mb_woven = late_in[:, (I + half) * PACK : (I + Q) * PACK]
        ma_woven = mb_woven
        ma_codes = sb.tile([P, EA], U32, name="ma_codes", align_bytes=64)
        ma_scales = sb.tile([P, EA], U8, name="ma_scales", align_bytes=64)
        mb_codes = sb.tile([P, E - EA], U32, name="mb_codes", align_bytes=64)
        mb_scales = sb.tile([P, E - EA], U8, name="mb_scales", align_bytes=64)

        gather_words(CH, I)
        nc.gpsimd.tensor_scalar(
            ma_woven.rearrange("p (e r) -> p e r", r=PACK), msgs_a[:].rearrange("p r e -> p e r"), 1.0, 0.0, MULT, ADD
        )
        nc.vector.quantize_mx(out=ma_codes[:].bitcast(FP8X4), scales=ma_scales[:], in_=ma_woven)
        nc.gpsimd.tensor_scalar(
            mb_woven.rearrange("p (e r) -> p e r", r=PACK), msgs_b[:].rearrange("p r e -> p e r"), 1.0, 0.0, MULT, ADD
        )

        def m_operand(j):
            if j * P < EA:
                return ma_codes[:, j * P : (j + 1) * P], ma_scales[:, j * P : (j + 1) * P]
            return mb_codes[:, j * P - EA : (j + 1) * P - EA], mb_scales[:, j * P - EA : (j + 1) * P - EA]

        dl_all = sb.tile([P, 3, I], F32, name="dl_all")
        dl_last = sb.tile([P, M], F32, name="dl_last")
        dl = [dl_all[:, 0, :], dl_all[:, 1, :], dl_all[:, 2, :], dl_last[:, 0:I]]
        stretch = {0: (0, 128), 1: (128, 256), 3: (256, 512)}

        def scatter(engine, j, a, b):
            window = placed[j][:].indirect(place_list[:, a // LIST : b // LIST])
            if engine == "s":
                nc.scalar.activation(window, dl[j % 2][:, a:b], COPY)
            else:
                nc.vector.tensor_copy(window, dl[j][:, a:b])

        w = sb.tile([P, NCH * CH * PACK], F32, name="w", tag="w_then_faded")
        w_codes = sb.tile([P, I], U32, name="w_codes", align_bytes=64)
        w_scales = sb.tile([P, I], U8, name="w_scales", align_bytes=64)
        for c in range(NCH):
            cols = slice(c * CH, (c + 1) * CH)
            s_bank = ps_s.tile([P, PACK, CH], F32, name="s_bank", tag="bank")
            for r in range(PACK):
                nc.tensor.matmul_mx(
                    out=s_bank[:, r, :],
                    lhsT=u_codes[:, r * P : (r + 1) * P].bitcast(FP8X4),
                    lhsT_scale=u_scales[:, r * P : (r + 1) * P],
                    rhs=got_words[:, cols].bitcast(FP8X4),
                    rhs_scale=got_bytes[:, cols],
                    start=True,
                    stop=True,
                )
            w_c = w[:, c * CH * PACK : (c + 1) * CH * PACK].rearrange("p (i r) -> p i r", r=PACK)
            nc.scalar.activation(w_c, s_bank[:].rearrange("p r i -> p i r"), SIGMOID)
            wq = late_in[:, c * CH * PACK : (c + 1) * CH * PACK]
            nc.vector.tensor_tensor(
                wq[:].rearrange("p (i r) -> p i r", r=PACK),
                w_c,
                qs_bank[:, 0:PACK].unsqueeze(1).to_broadcast([P, CH, PACK]),
                MULT,
            )
            if c in stretch:
                a, b = stretch[c]
                nc.vector.quantize_mx(
                    out=w_codes[:, a:b].bitcast(FP8X4), scales=w_scales[:, a:b], in_=late_in[:, a * PACK : b * PACK]
                )
                d_bank = ps_d.tile([P, 2, b - a], F32, name="d_bank")
                for j in range(2):
                    codes, scales = m_operand(j)
                    nc.tensor.matmul_mx(
                        out=d_bank[:, j, :],
                        lhsT=codes.bitcast(FP8X4),
                        lhsT_scale=scales,
                        rhs=w_codes[:, a:b].bitcast(FP8X4),
                        rhs_scale=w_scales[:, a:b],
                        start=True,
                        stop=True,
                    )
                nc.scalar.copy(dl_all[:, 0:2, a:b], d_bank[:])
                for j in range(2):
                    scatter("s", j, a, b)
            if c == 0 + 1:
                nc.vector.quantize_mx(out=mb_codes[:].bitcast(FP8X4), scales=mb_scales[:], in_=mb_woven[:])

        banks = {}
        for j in (3, 2):
            banks[j] = ps_s.tile([P, I], F32, name=f"d_whole{j}", tag="bank")
            codes, scales = m_operand(j)
            nc.tensor.matmul_mx(
                out=banks[j][:],
                lhsT=codes.bitcast(FP8X4),
                lhsT_scale=scales,
                rhs=w_codes[:].bitcast(FP8X4),
                rhs_scale=w_scales[:],
                start=True,
                stop=True,
            )

        faded_v = sb.tile([P, 2 * M], F32, name="faded_v", tag="w_then_faded")
        faded_g = sb.tile([P, 2 * M], F32, name="faded_g", tag="late_in_then_faded", align_bytes=64)
        faded = {3: faded_v[:, 0:M], 0: faded_v[:, M : 2 * M], 1: faded_g[:, 0:M], 2: faded_g[:, M : 2 * M], 4: dl_last[:], 5: old_sb[2][:]}

        def fade_tile(engine, j):
            if engine == "g":
                nc.gpsimd.tensor_tensor(faded[j], old_sb[j][:], fade_row[:], MULT)
                return
            for h in range(2):
                src = old_sb[j][:, h * 512 : (h + 1) * 512].rearrange("p (n c) -> p n c", c=PACK)
                dst = faded[j][:, h * 512 : (h + 1) * 512].rearrange("p (n c) -> p n c", c=PACK)
                nc.vector.tensor_tensor(dst, src, fade_bank[h][:].rearrange("p c n -> p n c"), MULT)

        def finish(engine, j, a, b, onto=None):
            eng = nc.gpsimd if engine == "g" else nc.vector
            result = old_sb[j][:, a:b] if onto is None else faded[onto][:, a:b]
            eng.tensor_tensor(result, faded[j][:, a:b], placed[j][:, a:b], ADD)
            nc.sync.dma_start(out[j * P : (j + 1) * P, a:b], result)

        for step in [
            ("fade", "g", 1), ("fade", "g", 2),
            ("fade", "v", 0), ("copy", "v", 3, 0, 512), ("copy", "v", 2, 0, 128), ("fade", "v", 3),
            ("scatter", "v", 2, 0, 128), ("scatter", "v", 3, 0, 512),
            ("copy", "s", 2, 128, 512), ("scatter", "s", 2, 128, 512),
            ("finish", "g", 0, 0, 1024, 5),
            ("finish", "v", 1, 0, 1024, 0), ("finish", "v", 3, 0, 512, 1), ("finish", "v", 3, 512, 1024, 1),
            ("finish", "v", 2, 0, 512, 3), ("finish", "v", 2, 512, 768, 3), ("finish", "v", 2, 768, 1024, 3),
        ]:
            if step[0] == "fade":
                fade_tile(*step[1:])
            elif step[0] == "copy":
                j, a, b = step[2:]
                if step[1] == "s":
                    nc.scalar.copy(dl[j % 2][:, a:b], banks[j][:, a:b])
                else:
                    nc.vector.tensor_copy(dl[j][:, a:b], banks[j][:, a:b])
            elif step[0] == "scatter":
                scatter(*step[1:])
            else:
                finish(*step[1:])
